import numpy as np
import ml_dtypes


def mxq(x, axis, fmt="e4m3"):
    dtype, down = {"e4m3": (ml_dtypes.float8_e4m3fn, 7), "e5m2": (ml_dtypes.float8_e5m2, 14)}[fmt]
    v = np.moveaxis(np.asarray(x, np.float32).astype(ml_dtypes.bfloat16).astype(np.float64), axis, -1)
    blocks = v.reshape(v.shape[:-1] + (-1, 32))
    amax = np.abs(blocks).max(-1, keepdims=True)
    byte = np.maximum(np.where(amax > 0, np.frexp(amax)[1] - 1 + 127, 0) - down, 1)
    scale = np.exp2(byte - 127.0)
    codes = (blocks / scale).astype(np.float32).astype(dtype).astype(np.float64)
    return np.moveaxis((codes * scale).reshape(v.shape), -1, axis)


WIDE = False


def mx_kscale(k):
    if not WIDE:
        return np.ones(k)
    levels = np.array([30, -30])
    if k % 512:
        return np.exp2(np.random.permutation(np.resize(levels, k // 32))).repeat(32)
    a = np.empty((k // 512, 16))
    for p in range(k // 512):
        a[p, :8] = np.random.permutation(np.resize(levels, 8))
        for g in range(8):
            far = levels[np.abs(levels - a[p, g]) >= 10]
            a[p, g + 8] = far[np.random.randint(len(far))]
    return np.exp2(a.ravel()).repeat(32)


def f64(x):
    return np.asarray(x).astype(np.float64)


def striped(idx):
    return np.tile(np.asarray(idx).reshape(-1, 16).T, (8, 1)).astype(np.uint16)


def unstriped(offs):
    return offs[:16].T.reshape(-1).astype(np.int64)


def striped8(idx):
    return np.asarray(idx).reshape(8, -1, 16).transpose(0, 2, 1).reshape(128, -1).astype(np.uint16)


def unstriped8(offs):
    return offs.reshape(8, 16, -1).transpose(0, 2, 1).reshape(8, -1).astype(np.int64)


def pick8(x, idx, run):
    r = np.arange(len(x))
    return x[r[:, None], idx[r % (8 * run) // run]]


E2M1 = np.array([0.0, 0.5, 1.0, 1.5, 2.0, 3.0, 4.0, 6.0, -0.0, -0.5, -1.0, -1.5, -2.0, -3.0, -4.0, -6.0])


def pack_weight(w, fmt):
    k, n = w.shape
    w = f64(np.asarray(w, np.float32).astype(ml_dtypes.bfloat16)).reshape(k // 32, 32, n)
    amax = np.abs(w).max(1)
    if fmt in ("e4m3", "e5m2"):
        byte = np.frexp(amax)[1] - 1 + 127 - (7 if fmt == "e4m3" else 14)
    else:
        mant, ex = np.frexp(amax / 6.0)
        byte = np.where(mant > 0.5, ex, ex - 1) + 127
    byte = np.clip(np.where(amax > 0, byte, 1), 1, 254)
    scaled = (w * np.exp2(127.0 - byte)[:, None, :]).reshape(k, n).astype(np.float32)
    by_word = np.ascontiguousarray(scaled.reshape(k // 512, 128, 4, n).transpose(0, 1, 3, 2))
    if fmt in ("e4m3", "e5m2"):
        words = by_word.astype(ml_dtypes.float8_e4m3fn if fmt == "e4m3" else ml_dtypes.float8_e5m2).view(np.uint8)
    else:
        c = by_word.astype(ml_dtypes.float4_e2m1fn).view(np.uint8) & 0xF
        words = (c[..., 0::2] | (c[..., 1::2] << 4)).reshape(k // 512, 128, 2 * n)
    return np.ascontiguousarray(words), np.ascontiguousarray(byte.astype(np.uint8).reshape(k // 512, 16, n))


def unpack_weight(words, scales, fmt):
    g, _, n = scales.shape
    words = np.ascontiguousarray(words).reshape(g, 128, n, -1)
    if fmt in ("e4m3", "e5m2"):
        vals = words.view(ml_dtypes.float8_e4m3fn if fmt == "e4m3" else ml_dtypes.float8_e5m2).astype(np.float64)
    else:
        nib = np.empty((g, 128, n, 4), np.uint8)
        nib[..., 0::2] = words & 0xF
        nib[..., 1::2] = words >> 4
        vals = E2M1[nib]
    vals = vals * np.repeat(np.exp2(scales.astype(np.float64) - 127.0), 8, axis=1)[..., None]
    return vals.transpose(0, 1, 3, 2).reshape(g * 512, n)


K, T, J, R, V, C, D, O, N, E = 512, 1024, 256, 512, 1024, 512, 512, 128, 256, 512


def setup_inputs():
    n = np.random.standard_normal
    idx = np.random.permutation(V)[:R]
    idx2 = np.random.permutation(T)[:J]
    idx3 = np.stack([np.random.permutation(C)[:J] for _ in range(8)])
    idx4 = np.stack([np.random.permutation(D)[:J] for _ in range(8)])
    idx5 = np.random.permutation(C)[:O]
    idx6 = np.random.permutation(D)[:O]
    idx7 = np.stack([np.random.permutation(E)[:O] for _ in range(8)])
    fk = mx_kscale(K)
    fr = mx_kscale(R)
    tr = np.ones(V)
    tr[idx] = fr
    xtp = pack_weight(n((K, T)) / fk[:, None], "e5m2")
    wtp = pack_weight(n((K, V)) * 1 / np.sqrt(K) * fk[:, None] * tr, "e2m1")
    wbp = pack_weight(n((R, N)) * 1 / np.sqrt(R) / fr[:, None], "e2m1")
    return {
        "xt_words": xtp[0],
        "xt_scales": xtp[1],
        "wt_words": wtp[0],
        "wt_scales": wtp[1],
        "sa": (np.random.uniform(0.5, 1.6, (R, 1))).astype(np.float32),
        "sb": (np.random.uniform(0.5, 1.6, (R, 1))).astype(np.float32),
        "wb_words": wbp[0],
        "wb_scales": wbp[1],
        "offs": striped(idx),
        "offs2": striped(idx2),
        "offs3": striped8(idx3),
        "offs4": striped8(idx4),
        "offs5": striped(idx5),
        "offs6": striped(idx6),
        "offs7": striped8(idx7),
    }


def reference(xt_words, xt_scales, wt_words, wt_scales, sa, sb, wb_words, wb_scales, offs, offs2, offs3, offs4, offs5, offs6, offs7):
    idx = unstriped(offs)
    idx2 = unstriped(offs2)
    idx3 = unstriped8(offs3)
    idx4 = unstriped8(offs4)
    idx5 = unstriped(offs5)
    idx6 = unstriped(offs6)
    idx7 = unstriped8(offs7)
    xtu = unpack_weight(xt_words, xt_scales, "e5m2")
    wtu = unpack_weight(wt_words, wt_scales, "e2m1")
    wbu = unpack_weight(wb_words, wb_scales, "e2m1")
    wtidxg = wtu[:, idx]
    xtidx2g = xtu[:, idx2]
    a = wtidxg.T @ xtidx2g
    pw = np.zeros((R, C))
    pw[np.arange(R)[:, None], idx3[np.arange(R) % 512 // 64]] = a
    pv = np.zeros((R, D))
    pv[np.arange(R)[:, None], idx4[np.arange(R) % 512 // 64]] = a
    hid = np.abs(pw[:, idx5] * f64(sa) - pv[:, idx6] * f64(sb))
    hidq = mxq(hid, 0, "e4m3")
    p = wbu.T @ hidq
    y = np.zeros((N, E))
    y[np.arange(N)[:, None], idx7[np.arange(N) % 128 // 16]] = p
    return y

@@ -1,0 +1,162 @@
+from contextlib import ExitStack
+
+import concourse.mybir as mybir
+
+K, T, J, R, V, C, D, O, N, E = 512, 1024, 256, 512, 1024, 512, 512, 128, 256, 512
+FLOPS = 2 * K * R * J + 2 * R * N * O
+
+F32 = mybir.dt.float32
+BF16 = mybir.dt.bfloat16
+I32 = mybir.dt.int32
+U32 = mybir.dt.uint32
+U16 = mybir.dt.uint16
+U8 = mybir.dt.uint8
+E4M3 = mybir.dt.float8_e4m3fn_x4
+E5M2 = mybir.dt.float8_e5m2_x4
+E2M1 = mybir.dt.float4_e2m1fn_x4
+ALU = mybir.AluOpType
+COPY = mybir.ActivationFunctionType.Copy
+
+P = 128
+PACK = 4
+HALF = J // 2
+
+
+def load_list(nc, pool, offs, name):
+    tile = pool.tile(list(offs.shape), U16, name=name)
+    nc.sync.dma_start(tile[:], offs)
+    return tile
+
+
+def load_scale_rows(queue, plane, scales):
+    for q in range(4):
+        queue.dma_start(plane[32 * q : 32 * q + 4, :].bitcast(I32), scales[0, 4 * q : 4 * q + 4, :].bitcast(I32))
+
+
+def tile_list_owntwice_chosen_one_ownpage_kernel(
+    tc, xt_words, xt_scales, wt_words, wt_scales, sa, sb, wb_words, wb_scales,
+    offs, offs2, offs3, offs4, offs5, offs6, offs7, out,
+):
+    nc = tc.nc
+    with ExitStack() as ctx:
+        lists = ctx.enter_context(tc.tile_pool(name="lists", bufs=1))
+        keep = ctx.enter_context(tc.tile_pool(name="keep", bufs=1))
+        psum = ctx.enter_context(tc.psum_pool(name="psum", bufs=1))
+
+        wt_plane = keep.tile([P, V], U8, align_bytes=64)
+        xt_plane = keep.tile([P, T], U8, align_bytes=64)
+        wb_plane = keep.tile([P, N], U8, align_bytes=64)
+        wt_table = keep.tile([P, V], U16, align_bytes=64)
+        xt_table = keep.tile([P, T], U32, align_bytes=64)
+        wb_codes = keep.tile([P, N], U16, align_bytes=64)
+        sa_sb = keep.tile([P, PACK], F32)
+        sb_sb = keep.tile([P, PACK], F32)
+        pw = keep.tile([P, C], F32)
+        pv = keep.tile([P, D], F32)
+
+        nc.vector.memset(wt_plane[:].bitcast(I32), 0)
+        nc.vector.memset(xt_plane[:].bitcast(I32), 0)
+        nc.vector.memset(pw[:].bitcast(I32), 0)
+        nc.vector.memset(pv[:].bitcast(I32), 0)
+        nc.vector.memset(wb_plane[:].bitcast(I32), 0)
+
+        l1 = load_list(nc, lists, offs, "l1")
+        nc.sync.dma_start(wt_table[:].bitcast(I32), wt_words[0].bitcast(I32))
+        load_scale_rows(nc.sync, wt_plane, wt_scales)
+        l2 = load_list(nc, lists, offs2, "l2")
+        nc.sync.dma_start(xt_table[:].bitcast(I32), xt_words[0].rearrange("p n t -> p (n t)").bitcast(I32))
+        load_scale_rows(nc.sync, xt_plane, xt_scales)
+        l3 = load_list(nc, lists, offs3, "l3")
+        l4 = load_list(nc, lists, offs4, "l4")
+        l5 = load_list(nc, lists, offs5, "l5")
+        l6 = load_list(nc, lists, offs6, "l6")
+        nc.sync.dma_start(sa_sb[:], sa.rearrange("(p t) o -> p (t o)", t=PACK))
+        nc.sync.dma_start(sb_sb[:], sb.rearrange("(p t) o -> p (t o)", t=PACK))
+        l7 = load_list(nc, lists, offs7, "l7")
+        nc.sync.dma_start(wb_codes[:].bitcast(I32), wb_words[0].bitcast(I32))
+        load_scale_rows(nc.sync, wb_plane, wb_scales)
+
+        wg_plane = keep.tile([P, R], U8, align_bytes=64)
+        wg_codes = keep.tile([P, R], U16, align_bytes=64)
+        xg_plane = keep.tile([P, J], U8, align_bytes=64)
+        xg_codes = keep.tile([P, J], U32, align_bytes=64)
+        nc.vector.tensor_copy(wg_codes[:], wt_table[:].indirect(l1[:]))
+        nc.vector.tensor_copy(wg_plane[:], wt_plane[:].indirect(l1[:]))
+
+        def deal(t):
+            codes = keep.tile([P, P], U16, align_bytes=64, name="wd_codes")
+            plane = keep.tile([P, P], U8, align_bytes=64, name="wd_plane")
+            nc.vector.tensor_copy(plane[:], wg_plane[:, t::PACK])
+            nc.vector.tensor_copy(codes[:], wg_codes[:, t::PACK])
+            return codes, plane
+
+        def gather_tokens(h):
+            cols = slice(h * HALF, (h + 1) * HALF)
+            entries = l2[:, h * HALF // 16 : (h + 1) * HALF // 16]
+            nc.vector.tensor_copy(xg_codes[:, cols], xt_table[:].indirect(entries))
+            nc.vector.tensor_copy(xg_plane[:, cols], xt_plane[:].indirect(entries))
+
+        def product(weights, cols, name):
+            codes, plane = weights
+            acc = psum.tile([P, cols.stop - cols.start], F32, name=name)
+            nc.tensor.matmul_mx(
+                acc[:], lhsT=codes[:].bitcast(E2M1), lhsT_scale=plane[:],
+                rhs=xg_codes[:, cols].bitcast(E5M2), rhs_scale=xg_plane[:, cols], start=True, stop=True,
+            )
+            return acc
+
+        a_sb = [keep.tile([P, J], F32, name="a%d" % t, tag="a%d" % t) for t in range(PACK)]
+        hid = keep.tile([P, O, PACK], BF16, align_bytes=64)
+
+        def place(t, cols):
+            entries = slice(cols.start // 16, cols.stop // 16)
+            nc.scalar.activation(pw[:].indirect(l3[:, entries]), a_sb[t][:, cols], COPY)
+            nc.scalar.activation(pv[:].indirect(l4[:, entries]), a_sb[t][:, cols], COPY)
+
+        def look(t):
+            gw = keep.tile([P, O], F32, name="gw%d" % t)
+            gv = keep.tile([P, O], F32, name="gv%d" % t)
+            diff = keep.tile([P, O], F32, name="diff%d" % t)
+            nc.scalar.activation(gw[:], pw[:].indirect(l5[:]), COPY, scale=sa_sb[:, t : t + 1])
+            nc.scalar.activation(gv[:], pv[:].indirect(l6[:]), COPY, scale=sb_sb[:, t : t + 1])
+            nc.vector.tensor_tensor(diff[:], gw[:], gv[:], ALU.subtract)
+            nc.vector.scalar_tensor_tensor(hid[:, :, t], diff[:], -1.0, diff[:], ALU.mult, ALU.max)
+
+        first, second, whole = slice(0, HALF), slice(HALF, J), slice(0, J)
+        w0 = deal(0)
+        gather_tokens(0)
+        acc = product(w0, first, "acc0a")
+        nc.scalar.copy(a_sb[0][:, first], acc[:])
+        place(0, first)
+        gather_tokens(1)
+        acc = product(w0, second, "acc0b")
+        nc.vector.tensor_copy(a_sb[0][:, second], acc[:])
+        place(0, second)
+        for t in range(1, PACK):
+            acc = product(deal(t), whole, "acc%d" % t)
+            nc.vector.tensor_copy(a_sb[t][:], acc[:])
+        look(0)
+        for t in range(1, PACK):
+            place(t, whole)
+            look(t)
+
+        pages = [keep.tile([P, E], F32, name="page%d" % h, tag="a%d" % h) for h in range(N // P)]
+        for page in pages:
+            nc.vector.memset(page[:], 0.0)
+        hq_codes = keep.tile([P, O], U32, align_bytes=64)
+        hq_plane = keep.tile([P, O], U8, align_bytes=64)
+        nc.vector.quantize_mx(hq_codes[:].bitcast(E4M3), hq_plane[:], hid[:].rearrange("p o t -> p (o t)"))
+        for h in range(N // P):
+            cols = slice(h * P, (h + 1) * P)
+            acc = psum.tile([P, O], F32, name="res%d" % h)
+            nc.tensor.matmul_mx(
+                acc[:], lhsT=wb_codes[:, cols].bitcast(E2M1), lhsT_scale=wb_plane[:, cols],
+                rhs=hq_codes[:].bitcast(E4M3), rhs_scale=hq_plane[:], start=True, stop=True,
+            )
+            p_sb = keep.tile([P, O], F32, name="p%d" % h)
+            if h == 0:
+                nc.scalar.copy(p_sb[:], acc[:])
+            else:
+                nc.vector.tensor_copy(p_sb[:], acc[:])
+            nc.scalar.activation(pages[h][:].indirect(l7[:]), p_sb[:], COPY)
+            nc.sync.dma_start(out[cols, :], pages[h][:])

@@ -43,7 +43,7 @@ def tile_list_owntwice_chosen_one_ownpage_kernel(
         keep = ctx.enter_context(tc.tile_pool(name="keep", bufs=1))
         psum = ctx.enter_context(tc.psum_pool(name="psum", bufs=1))
 
-        wt_plane = keep.tile([P, V], U8, align_bytes=64)
+        wt_plane = keep.tile([P, V], U8, align_bytes=64, tag="wt_plane")
         xt_plane = keep.tile([P, T], U8, align_bytes=64)
         wb_plane = keep.tile([P, N], U8, align_bytes=64)
         wt_table = keep.tile([P, V], U16, align_bytes=64)
@@ -63,10 +63,10 @@ def tile_list_owntwice_chosen_one_ownpage_kernel(
         l1 = load_list(nc, lists, offs, "l1")
         nc.sync.dma_start(wt_table[:].bitcast(I32), wt_words[0].bitcast(I32))
         load_scale_rows(nc.sync, wt_plane, wt_scales)
-        l2 = load_list(nc, lists, offs2, "l2")
+        l3 = load_list(nc, lists, offs3, "l3")
         nc.sync.dma_start(xt_table[:].bitcast(I32), xt_words[0].rearrange("p n t -> p (n t)").bitcast(I32))
         load_scale_rows(nc.sync, xt_plane, xt_scales)
-        l3 = load_list(nc, lists, offs3, "l3")
+        l2 = load_list(nc, lists, offs2, "l2")
         l4 = load_list(nc, lists, offs4, "l4")
         l5 = load_list(nc, lists, offs5, "l5")
         l6 = load_list(nc, lists, offs6, "l6")
@@ -84,10 +84,10 @@ def tile_list_owntwice_chosen_one_ownpage_kernel(
         nc.vector.tensor_copy(wg_plane[:], wt_plane[:].indirect(l1[:]))
 
         def deal(t):
-            codes = keep.tile([P, P], U16, align_bytes=64, name="wd_codes")
+            codes = keep.tile([P, P], U16, align_bytes=64, name="wd_codes", tag="wt_plane")
             plane = keep.tile([P, P], U8, align_bytes=64, name="wd_plane")
-            nc.vector.tensor_copy(plane[:], wg_plane[:, t::PACK])
             nc.vector.tensor_copy(codes[:], wg_codes[:, t::PACK])
+            nc.vector.tensor_copy(plane[:], wg_plane[:, t::PACK])
             return codes, plane
 
         def gather_tokens(h):
@@ -113,14 +113,18 @@ def tile_list_owntwice_chosen_one_ownpage_kernel(
             nc.scalar.activation(pw[:].indirect(l3[:, entries]), a_sb[t][:, cols], COPY)
             nc.scalar.activation(pv[:].indirect(l4[:, entries]), a_sb[t][:, cols], COPY)
 
-        def look(t):
+        def look(t, parts):
             gw = keep.tile([P, O], F32, name="gw%d" % t)
             gv = keep.tile([P, O], F32, name="gv%d" % t)
             diff = keep.tile([P, O], F32, name="diff%d" % t)
             nc.scalar.activation(gw[:], pw[:].indirect(l5[:]), COPY, scale=sa_sb[:, t : t + 1])
-            nc.scalar.activation(gv[:], pv[:].indirect(l6[:]), COPY, scale=sb_sb[:, t : t + 1])
-            nc.vector.tensor_tensor(diff[:], gw[:], gv[:], ALU.subtract)
-            nc.vector.scalar_tensor_tensor(hid[:, :, t], diff[:], -1.0, diff[:], ALU.mult, ALU.max)
+            for cols in parts:
+                entries = l6[:, cols.start // 16 : cols.stop // 16]
+                nc.scalar.activation(gv[:, cols], pv[:].indirect(entries), COPY, scale=sb_sb[:, t : t + 1])
+            for cols in parts:
+                nc.vector.tensor_tensor(diff[:, cols], gw[:, cols], gv[:, cols], ALU.subtract)
+            for cols in parts:
+                nc.vector.scalar_tensor_tensor(hid[:, cols, t], diff[:, cols], -1.0, diff[:, cols], ALU.mult, ALU.max)
 
         first, second, whole = slice(0, HALF), slice(HALF, J), slice(0, J)
         w0 = deal(0)
@@ -135,17 +139,19 @@ def tile_list_owntwice_chosen_one_ownpage_kernel(
         for t in range(1, PACK):
             acc = product(deal(t), whole, "acc%d" % t)
             nc.vector.tensor_copy(a_sb[t][:], acc[:])
-        look(0)
+        halves = [slice(0, O // 2), slice(O // 2, O)]
+        look(0, [slice(0, O)])
         for t in range(1, PACK):
             place(t, whole)
-            look(t)
+            look(t, halves if t == PACK - 1 else [slice(0, O)])
 
         pages = [keep.tile([P, E], F32, name="page%d" % h, tag="a%d" % h) for h in range(N // P)]
         for page in pages:
             nc.vector.memset(page[:], 0.0)
         hq_codes = keep.tile([P, O], U32, align_bytes=64)
         hq_plane = keep.tile([P, O], U8, align_bytes=64)
-        nc.vector.quantize_mx(hq_codes[:].bitcast(E4M3), hq_plane[:], hid[:].rearrange("p o t -> p (o t)"))
+        for cols in halves:
+            nc.vector.quantize_mx(hq_codes[:, cols].bitcast(E4M3), hq_plane[:, cols], hid[:, cols, :].rearrange("p o t -> p (o t)"))
         for h in range(N // P):
             cols = slice(h * P, (h + 1) * P)
             acc = psum.tile([P, O], F32, name="res%d" % h)

from contextlib import ExitStack

import concourse.mybir as mybir

K, T, J, R, V, C, D, O, N, E = 512, 1024, 256, 512, 1024, 512, 512, 128, 256, 512
FLOPS = 2 * K * R * J + 2 * R * N * O

F32 = mybir.dt.float32
BF16 = mybir.dt.bfloat16
I32 = mybir.dt.int32
U32 = mybir.dt.uint32
U16 = mybir.dt.uint16
U8 = mybir.dt.uint8
E4M3 = mybir.dt.float8_e4m3fn_x4
E5M2 = mybir.dt.float8_e5m2_x4
E2M1 = mybir.dt.float4_e2m1fn_x4
ALU = mybir.AluOpType
COPY = mybir.ActivationFunctionType.Copy

P = 128
PACK = 4
HALF = J // 2


def load_list(nc, pool, offs, name):
    tile = pool.tile(list(offs.shape), U16, name=name)
    nc.sync.dma_start(tile[:], offs)
    return tile


def load_scale_rows(queue, plane, scales):
    for q in range(4):
        queue.dma_start(plane[32 * q : 32 * q + 4, :].bitcast(I32), scales[0, 4 * q : 4 * q + 4, :].bitcast(I32))


def tile_list_owntwice_chosen_one_ownpage_kernel(
    tc, xt_words, xt_scales, wt_words, wt_scales, sa, sb, wb_words, wb_scales,
    offs, offs2, offs3, offs4, offs5, offs6, offs7, out,
):
    nc = tc.nc
    with ExitStack() as ctx:
        lists = ctx.enter_context(tc.tile_pool(name="lists", bufs=1))
        keep = ctx.enter_context(tc.tile_pool(name="keep", bufs=1))
        psum = ctx.enter_context(tc.psum_pool(name="psum", bufs=1))

        wt_plane = keep.tile([P, V], U8, align_bytes=64, tag="wt_plane")
        xt_plane = keep.tile([P, T], U8, align_bytes=64)
        wb_plane = keep.tile([P, N], U8, align_bytes=64)
        wt_table = keep.tile([P, V], U16, align_bytes=64)
        xt_table = keep.tile([P, T], U32, align_bytes=64)
        wb_codes = keep.tile([P, N], U16, align_bytes=64)
        sa_sb = keep.tile([P, PACK], F32)
        sb_sb = keep.tile([P, PACK], F32)
        pw = keep.tile([P, C], F32)
        pv = keep.tile([P, D], F32)

        nc.vector.memset(wt_plane[:].bitcast(I32), 0)
        nc.vector.memset(xt_plane[:].bitcast(I32), 0)
        nc.vector.memset(pw[:].bitcast(I32), 0)
        nc.vector.memset(pv[:].bitcast(I32), 0)
        nc.vector.memset(wb_plane[:].bitcast(I32), 0)

        l1 = load_list(nc, lists, offs, "l1")
        nc.sync.dma_start(wt_table[:].bitcast(I32), wt_words[0].bitcast(I32))
        load_scale_rows(nc.sync, wt_plane, wt_scales)
        l3 = load_list(nc, lists, offs3, "l3")
        nc.sync.dma_start(xt_table[:].bitcast(I32), xt_words[0].rearrange("p n t -> p (n t)").bitcast(I32))
        load_scale_rows(nc.sync, xt_plane, xt_scales)
        l2 = load_list(nc, lists, offs2, "l2")
        l4 = load_list(nc, lists, offs4, "l4")
        l5 = load_list(nc, lists, offs5, "l5")
        l6 = load_list(nc, lists, offs6, "l6")
        nc.sync.dma_start(sa_sb[:], sa.rearrange("(p t) o -> p (t o)", t=PACK))
        nc.sync.dma_start(sb_sb[:], sb.rearrange("(p t) o -> p (t o)", t=PACK))
        l7 = load_list(nc, lists, offs7, "l7")
        nc.sync.dma_start(wb_codes[:].bitcast(I32), wb_words[0].bitcast(I32))
        load_scale_rows(nc.sync, wb_plane, wb_scales)

        wg_plane = keep.tile([P, R], U8, align_bytes=64)
        wg_codes = keep.tile([P, R], U16, align_bytes=64)
        xg_plane = keep.tile([P, J], U8, align_bytes=64)
        xg_codes = keep.tile([P, J], U32, align_bytes=64)
        nc.vector.tensor_copy(wg_codes[:], wt_table[:].indirect(l1[:]))
        nc.vector.tensor_copy(wg_plane[:], wt_plane[:].indirect(l1[:]))

        def deal(t):
            codes = keep.tile([P, P], U16, align_bytes=64, name="wd_codes", tag="wt_plane")
            plane = keep.tile([P, P], U8, align_bytes=64, name="wd_plane")
            nc.vector.tensor_copy(codes[:], wg_codes[:, t::PACK])
            nc.vector.tensor_copy(plane[:], wg_plane[:, t::PACK])
            return codes, plane

        def gather_tokens(h):
            cols = slice(h * HALF, (h + 1) * HALF)
            entries = l2[:, h * HALF // 16 : (h + 1) * HALF // 16]
            nc.vector.tensor_copy(xg_codes[:, cols], xt_table[:].indirect(entries))
            nc.vector.tensor_copy(xg_plane[:, cols], xt_plane[:].indirect(entries))

        def product(weights, cols, name):
            codes, plane = weights
            acc = psum.tile([P, cols.stop - cols.start], F32, name=name)
            nc.tensor.matmul_mx(
                acc[:], lhsT=codes[:].bitcast(E2M1), lhsT_scale=plane[:],
                rhs=xg_codes[:, cols].bitcast(E5M2), rhs_scale=xg_plane[:, cols], start=True, stop=True,
            )
            return acc

        a_sb = [keep.tile([P, J], F32, name="a%d" % t, tag="a%d" % t) for t in range(PACK)]
        hid = keep.tile([P, O, PACK], BF16, align_bytes=64)

        def place(t, cols):
            entries = slice(cols.start // 16, cols.stop // 16)
            nc.scalar.activation(pw[:].indirect(l3[:, entries]), a_sb[t][:, cols], COPY)
            nc.scalar.activation(pv[:].indirect(l4[:, entries]), a_sb[t][:, cols], COPY)

        def look(t, parts):
            gw = keep.tile([P, O], F32, name="gw%d" % t)
            gv = keep.tile([P, O], F32, name="gv%d" % t)
            diff = keep.tile([P, O], F32, name="diff%d" % t)
            nc.scalar.activation(gw[:], pw[:].indirect(l5[:]), COPY, scale=sa_sb[:, t : t + 1])
            for cols in parts:
                entries = l6[:, cols.start // 16 : cols.stop // 16]
                nc.scalar.activation(gv[:, cols], pv[:].indirect(entries), COPY, scale=sb_sb[:, t : t + 1])
            for cols in parts:
                nc.vector.tensor_tensor(diff[:, cols], gw[:, cols], gv[:, cols], ALU.subtract)
            for cols in parts:
                nc.vector.scalar_tensor_tensor(hid[:, cols, t], diff[:, cols], -1.0, diff[:, cols], ALU.mult, ALU.max)

        first, second, whole = slice(0, HALF), slice(HALF, J), slice(0, J)
        w0 = deal(0)
        gather_tokens(0)
        acc = product(w0, first, "acc0a")
        nc.scalar.copy(a_sb[0][:, first], acc[:])
        place(0, first)
        gather_tokens(1)
        acc = product(w0, second, "acc0b")
        nc.vector.tensor_copy(a_sb[0][:, second], acc[:])
        place(0, second)
        for t in range(1, PACK):
            acc = product(deal(t), whole, "acc%d" % t)
            nc.vector.tensor_copy(a_sb[t][:], acc[:])
        halves = [slice(0, O // 2), slice(O // 2, O)]
        look(0, [slice(0, O)])
        for t in range(1, PACK):
            place(t, whole)
            look(t, halves if t == PACK - 1 else [slice(0, O)])

        pages = [keep.tile([P, E], F32, name="page%d" % h, tag="a%d" % h) for h in range(N // P)]
        for page in pages:
            nc.vector.memset(page[:], 0.0)
        hq_codes = keep.tile([P, O], U32, align_bytes=64)
        hq_plane = keep.tile([P, O], U8, align_bytes=64)
        for cols in halves:
            nc.vector.quantize_mx(hq_codes[:, cols].bitcast(E4M3), hq_plane[:, cols], hid[:, cols, :].rearrange("p o t -> p (o t)"))
        for h in range(N // P):
            cols = slice(h * P, (h + 1) * P)
            acc = psum.tile([P, O], F32, name="res%d" % h)
            nc.tensor.matmul_mx(
                acc[:], lhsT=wb_codes[:, cols].bitcast(E2M1), lhsT_scale=wb_plane[:, cols],
                rhs=hq_codes[:].bitcast(E4M3), rhs_scale=hq_plane[:], start=True, stop=True,
            )
            p_sb = keep.tile([P, O], F32, name="p%d" % h)
            if h == 0:
                nc.scalar.copy(p_sb[:], acc[:])
            else:
                nc.vector.tensor_copy(p_sb[:], acc[:])
            nc.scalar.activation(pages[h][:].indirect(l7[:]), p_sb[:], COPY)
            nc.sync.dma_start(out[cols, :], pages[h][:])
